import numpy as np
import ml_dtypes


def mxq(x, axis, fmt="e4m3"):
    dtype, down = {"e4m3": (ml_dtypes.float8_e4m3fn, 7), "e5m2": (ml_dtypes.float8_e5m2, 14)}[fmt]
    v = np.moveaxis(np.asarray(x, np.float32).astype(ml_dtypes.bfloat16).astype(np.float64), axis, -1)
    blocks = v.reshape(v.shape[:-1] + (-1, 32))
    amax = np.abs(blocks).max(-1, keepdims=True)
    byte = np.maximum(np.where(amax > 0, np.frexp(amax)[1] - 1 + 127, 0) - down, 1)
    scale = np.exp2(byte - 127.0)
    codes = (blocks / scale).astype(np.float32).astype(dtype).astype(np.float64)
    return np.moveaxis((codes * scale).reshape(v.shape), -1, axis)


WIDE = False


def mx_kscale(k):
    if not WIDE:
        return np.ones(k)
    levels = np.array([10, -10, 5, -5, 0])
    if k % 512:
        return np.exp2(np.random.permutation(np.resize(levels, k // 32))).repeat(32)
    a = np.empty((k // 512, 16))
    for p in range(k // 512):
        a[p, :8] = np.random.permutation(np.resize(levels, 8))
        for g in range(8):
            far = levels[np.abs(levels - a[p, g]) >= 10]
            a[p, g + 8] = far[np.random.randint(len(far))]
    return np.exp2(a.ravel()).repeat(32)


def f64(x):
    return np.asarray(x).astype(np.float64)


def striped(idx):
    return np.tile(idx.reshape(-1, 16).T, (8, 1)).astype(np.uint16)


def unstriped(offs):
    return offs[:16].T.reshape(-1).astype(np.int64)


def striped8(idx):
    return np.concatenate([x.reshape(-1, 16).T for x in idx]).astype(np.uint16)


def runs(offs, k):
    lists = np.stack([offs[16 * r : 16 * r + 16].T.reshape(-1) for r in range(8)]).astype(np.int64)
    return lists[np.arange(k) % 512 // 64]


def pack_weight(w):
    k, n = w.shape
    w = f64(np.asarray(w, np.float32).astype(ml_dtypes.bfloat16)).reshape(k // 32, 32, n)
    amax = np.abs(w).max(1)
    byte = np.clip(np.where(amax > 0, np.frexp(amax)[1] - 1 + 127 - 7, 1), 1, 254)
    scaled = (w * np.exp2(127.0 - byte)[:, None, :]).reshape(k, n).astype(np.float32)
    words = np.ascontiguousarray(scaled.reshape(k // 512, 128, 4, n).transpose(0, 1, 3, 2)).astype(ml_dtypes.float8_e4m3fn).view(np.uint8)
    return words, np.ascontiguousarray(byte.astype(np.uint8).reshape(k // 512, 16, n))


def unpack_weight(words, scales):
    g, p, n, _ = words.shape
    vals = np.ascontiguousarray(words).view(ml_dtypes.float8_e4m3fn).astype(np.float64) * np.repeat(np.exp2(scales.astype(np.float64) - 127.0), 8, axis=1)[..., None]
    return vals.transpose(0, 1, 3, 2).reshape(g * 512, n)


def sigmoid(v):
    return 1.0 / (1.0 + np.exp(-np.maximum(v, -700.0)))


K, T, S, N, H, U = 512, 2048, 512, 512, 512, 1024


def setup_inputs():
    n = np.random.standard_normal
    s = mx_kscale(K)[:, None]
    u = mx_kscale(S)
    packed_xT = pack_weight(n((K, T)) * s)
    return {
        "x_words": packed_xT[0],
        "x_scales": packed_xT[1],
        "wa": (n((K, H)) / np.sqrt(K) / s).astype(np.float32),
        "wb": (n((K, N)) / np.sqrt(K) / s).astype(np.float32),
        "tau": np.random.uniform(0.3, 0.9, (S, 1)).astype(np.float32),
        "gt": (np.random.uniform(0.5, 1.5, (S, 1)) * u[:, None]).astype(np.float32),
        "gi": (np.random.uniform(0.5, 1.5, (S, 1)) / u[:, None]).astype(np.float32),
        "mem": n((H, U)).astype(np.float32),
        "sl": np.random.uniform(1.0, 2.0, (H, 1)).astype(np.float32),
        "th": (0.5 * n((H, 1))).astype(np.float32),
        "offs": striped(np.random.permutation(T)[:S]),
        "two": striped(np.random.permutation(T)[:S]),
        "n1": striped8(np.stack([np.random.permutation(H) for _ in range(8)])),
        "n2": striped(np.random.permutation(U)[:N]),
        "n3": striped(np.random.permutation(N)),
    }


def reference(x_words, x_scales, wa, wb, tau, gt, gi, mem, sl, th, offs, two, n1, n2, n3):
    old = f64(mem)[:, unstriped(n2)]
    xq = unpack_weight(x_words, x_scales)[:, unstriped(offs)]
    a = xq.T @ mxq(f64(wa), 0, "e4m3")
    top = a.max(axis=1, keepdims=True)
    own = np.exp(f64(tau) * (a - top))
    ea = np.exp(f64(tau) * (a[np.arange(S)[:, None], runs(n1, S)] - top))
    z = f64(gt) * ((2.0 * (a * own)) / (own + ea + 0.25))
    x_two = unpack_weight(x_words, x_scales)[:, unstriped(two)]
    b = x_two.T @ mxq(f64(wb), 0, "e4m3")
    z2 = f64(gi) * b
    cv = 0.0625 * ((mxq(z, 0, "e4m3").T @ mxq(z2, 0, "e4m3")))
    sg = sigmoid(f64(sl) * (cv[:, unstriped(n3)] - f64(th)))
    nw = old + sg * (cv - old)
    out = f64(mem).copy()
    out[:, unstriped(n2)] = nw
    return out

@@ -1,0 +1,247 @@
+from contextlib import ExitStack
+
+import concourse.mybir as mybir
+
+K, T, S, N, H, U = 512, 2048, 512, 512, 512, 1024
+FLOPS = 2 * K * S * H + 2 * K * S * N + 2 * S * H * N
+
+F32 = mybir.dt.float32
+BF16 = mybir.dt.bfloat16
+I32 = mybir.dt.int32
+U32 = mybir.dt.uint32
+U16 = mybir.dt.uint16
+U8 = mybir.dt.uint8
+FP8X4 = mybir.dt.float8_e4m3fn_x4
+ALU = mybir.AluOpType
+ACT = mybir.ActivationFunctionType
+
+P = 128
+PACK = 4
+HALF = 256
+LIST_COLS = 32
+HALF_COLS = 16
+
+
+def tile_picked_momeshepg_none_p_kernel(
+    tc, x_words, x_scales, wa, wb, tau, gt, gi, mem, sl, th, offs, two, n1, n2, n3, out
+):
+    nc = tc.nc
+    with ExitStack() as ctx:
+        keep = ctx.enter_context(tc.tile_pool(name="keep", bufs=1))
+        psum = ctx.enter_context(tc.psum_pool(name="psum", bufs=1))
+
+        def load_list(name, src):
+            t = keep.tile([P, LIST_COLS], U16, name=name)
+            nc.sync.dma_start(t[:], src)
+            return t
+
+        def load_by_token(name, src):
+            t = keep.tile([P, PACK], F32, name=name)
+            nc.sync.dma_start(t[:], src.rearrange("(p t) o -> p (t o)", t=PACK))
+            return t
+
+        def load_by_row(name, src):
+            t = keep.tile([P, PACK], F32, name=name)
+            with nc.allow_non_contiguous_dma(reason="one value a partition and row block"):
+                nc.sync.dma_start(t[:], src.rearrange("(i p) o -> p (i o)", p=P))
+            return t
+
+        def load_weight(name, src, cols):
+            t = keep.tile([P, PACK, cols.stop - cols.start], F32, name=name)
+            nc.sync.dma_start(t[:], src.rearrange("(p j) c -> p j c", j=PACK)[:, :, cols])
+            return t
+
+        def load_page(i):
+            t = keep.tile([P, U], F32, name="page%d" % i)
+            nc.sync.dma_start(t[:], mem[i * P : (i + 1) * P, :])
+            return t
+
+        offs_t = load_list("offs_t", offs)
+        two_t = load_list("two_t", two)
+        n2_t = load_list("n2_t", n2)
+        n1_t = load_list("n1_t", n1)
+        words = keep.tile([P, T], I32, name="words")
+        nc.sync.dma_start(words[:], x_words[0].rearrange("p c r -> p (c r)").bitcast(I32))
+        sbytes = keep.tile([P, T], U8, name="sbytes")
+        nc.gpsimd.memset(sbytes[:].bitcast(I32), 0)
+        for q in range(4):
+            nc.scalar.dma_start(
+                sbytes[32 * q : 32 * q + 4, :].bitcast(I32), x_scales[0, 4 * q : 4 * q + 4, :].bitcast(I32)
+            )
+        wa_raw = [load_weight("wa_raw%d" % u, wa, slice(u * HALF, (u + 1) * HALF)) for u in range(2)]
+        pages = [load_page(0)]
+        tau_t = load_by_token("tau_t", tau)
+        wb_raw = load_weight("wb_raw", wb, slice(0, N))
+        gt_t = load_by_token("gt_t", gt)
+        gi_t = load_by_token("gi_t", gi)
+        pages.extend(load_page(i) for i in range(1, 4))
+        n3_t = load_list("n3_t", n3)
+        sl_t = load_by_row("sl_t", sl)
+        th_t = load_by_row("th_t", th)
+
+        def pick_scales(name, lst):
+            scales = keep.tile([P, S], U8, name=name, align_bytes=64)
+            nc.vector.tensor_copy(
+                scales[:].rearrange("p (t m) -> p m t", t=PACK), sbytes[:].indirect(lst[:])
+            )
+            return scales
+
+        def pick_codes(name, lst, tag):
+            codes = keep.tile([P, S], U32, name=name, tag=tag, align_bytes=64)
+            nc.vector.tensor_copy(
+                codes[:].rearrange("p (t m) -> p m t", t=PACK), words[:].bitcast(U32).indirect(lst[:])
+            )
+            return codes
+
+        def round_on_gpsimd(dst, src):
+            nc.gpsimd.tensor_scalar(dst, src, 1.0, 0.0, ALU.mult, ALU.add)
+
+        def weave(name, raw, copy):
+            width = raw.shape[2]
+            woven = keep.tile([P, width * PACK], BF16, name=name, align_bytes=64)
+            copy(
+                woven[:].rearrange("p (c i j) -> p c j i", i=2, j=PACK),
+                raw[:].rearrange("p j (c i) -> p c j i", i=2),
+            )
+            return woven
+
+        def quantize(name, woven):
+            width = woven.shape[1] // PACK
+            codes = keep.tile([P, width], U32, name=name + "_codes", align_bytes=64)
+            scales = keep.tile([P, width], U8, name=name + "_scales", align_bytes=64)
+            nc.vector.quantize_mx(out=codes[:].bitcast(FP8X4), scales=scales[:], in_=woven[:])
+            return codes, scales
+
+        def product(dst, lhs, lcols, rhs, rcols):
+            nc.tensor.matmul_mx(
+                out=dst,
+                lhsT=lhs[0][:, lcols].bitcast(FP8X4),
+                lhsT_scale=lhs[1][:, lcols],
+                rhs=rhs[0][:, rcols].bitcast(FP8X4),
+                rhs_scale=rhs[1][:, rcols],
+                start=True,
+                stop=True,
+            )
+
+        def block(i):
+            return slice(i * P, (i + 1) * P)
+
+        def half(u):
+            return slice(u * HALF, (u + 1) * HALF)
+
+        def half_list(lst, u):
+            return lst[:, u * HALF_COLS : (u + 1) * HALF_COLS]
+
+        xa_scales = pick_scales("xa_scales", offs_t)
+        xa = (pick_codes("xa_codes", offs_t, "xa_codes"), xa_scales)
+        wa_woven = [weave("wa_woven0", wa_raw[0], nc.scalar.copy), weave("wa_woven1", wa_raw[1], nc.vector.tensor_copy)]
+        wa_q = [quantize("wa%d" % u, wa_woven[u]) for u in range(2)]
+
+        xb_scales = pick_scales("xb_scales", two_t)
+        old = [keep.tile([P, N], F32, name="old0")]
+        nc.scalar.activation(old[0][:], pages[0][:].indirect(n2_t[:]), ACT.Copy)
+
+        top = keep.tile([P, PACK], F32, name="top", tag="top", align_bytes=64)
+        shift = keep.tile([P, PACK], F32, name="shift")
+        ea = keep.tile([P, PACK, H], F32, name="ea")
+        a = []
+        for t in range(PACK):
+            bank = psum.tile([P, H], F32, name="a_bank%d" % t, tag="wide%d" % t)
+            for u in range(2):
+                product(bank[:, half(u)], xa, block(t), wa_q[u], slice(0, HALF))
+            a_t = keep.tile([P, H], F32, name="a%d" % t)
+            nc.vector.tensor_scalar(
+                a_t[:], bank[:], 1.0, None, ALU.mult, ALU.max, accum_out=top[:, t : t + 1]
+            )
+            nc.vector.tensor_scalar(
+                shift[:, t : t + 1], top[:, t : t + 1], tau_t[:, t : t + 1], -1.0, ALU.mult, ALU.mult
+            )
+            for u in range(2):
+                nc.scalar.activation(
+                    ea[:, t, half(u)],
+                    a_t[:].indirect(half_list(n1_t, u)),
+                    ACT.Exp,
+                    bias=shift[:, t : t + 1],
+                    scale=tau_t[:, t : t + 1],
+                )
+            a.append(a_t)
+
+        rest = keep.tile([P, PACK, H], F32, name="rest")
+        nc.scalar.activation(rest[:], ea[:], ACT.Ln, bias=0.25)
+
+        xb = (pick_codes("xb_codes", two_t, "top"), xb_scales)
+        wb_q = quantize("wb", weave("wb_woven", wb_raw, round_on_gpsimd))
+        ga = keep.tile([P, PACK, H], F32, name="ga")
+        for t in range(PACK):
+            nc.gpsimd.tensor_scalar(ga[:, t, :], a[t][:], gt_t[:, t : t + 1], 2.0, ALU.mult, ALU.mult)
+
+        logit = keep.tile([P, PACK, H], F32, name="logit", tag="logit")
+        share = keep.tile([P, PACK, H], F32, name="share")
+        for t in range(PACK):
+            nc.vector.scalar_tensor_tensor(
+                logit[:, t, :], a[t][:], tau_t[:, t : t + 1], rest[:, t, :], ALU.mult, ALU.subtract
+            )
+            nc.scalar.activation(share[:, t, :], logit[:, t, :], ACT.Sigmoid, bias=shift[:, t : t + 1])
+
+        z2_woven = keep.tile([P, N * PACK], BF16, name="z2_woven", align_bytes=64)
+        for i in range(4):
+            bank = psum.tile([P, PACK, P], F32, name="b_bank%d" % i)
+            for t in range(PACK):
+                product(bank[:, t, :], xb, block(t), wb_q, block(i))
+            nc.vector.tensor_tensor(
+                z2_woven[:, i * P * PACK : (i + 1) * P * PACK].rearrange("p (n t) -> p n t", t=PACK),
+                bank[:].rearrange("p t n -> p n t"),
+                gi_t[:].unsqueeze(1).broadcast_to([P, P, PACK]),
+                ALU.mult,
+            )
+        z2_q = quantize("z2", z2_woven)
+
+        old_rest = keep.tile([P, 3, N], F32, name="old_rest", tag="logit")
+        for i in range(1, 4):
+            nc.scalar.activation(old_rest[:, i - 1, :], pages[i][:].indirect(n2_t[:]), ACT.Copy)
+            old.append(old_rest[:, i - 1, :])
+
+        gate_bias = keep.tile([P, PACK], F32, name="gate_bias")
+        slope_th = keep.tile([P, PACK], F32, name="slope_th")
+        nc.gpsimd.tensor_tensor(slope_th[:], sl_t[:], th_t[:], ALU.mult)
+        nc.gpsimd.tensor_scalar(gate_bias[:], slope_th[:], -1.0, 0.0, ALU.mult, ALU.add)
+
+        cv_banks = []
+        cv = []
+        sg = []
+        for i in range(4):
+            z_woven = keep.tile([P, P * PACK], BF16, name="z_woven%d" % i, align_bytes=64)
+            nc.vector.tensor_tensor(
+                z_woven[:].rearrange("p (c e t) -> p c t e", e=2, t=PACK),
+                ga[:, :, block(i)].rearrange("p t (c e) -> p c t e", e=2),
+                share[:, :, block(i)].rearrange("p t (c e) -> p c t e", e=2),
+                ALU.mult,
+            )
+            z_q = quantize("z_block%d" % i, z_woven)
+            bank = psum.tile([P, N], F32, name="cv_bank%d" % i, tag="wide%d" % i)
+            product(bank[:], z_q, slice(0, P), z2_q, slice(0, N))
+            cv_banks.append(bank)
+        for i in range(4):
+            cv_i = keep.tile([P, N], F32, name="cv%d" % i)
+            nc.vector.tensor_scalar(cv_i[:], cv_banks[i][:], 0.0625, None, ALU.mult)
+            sg_i = keep.tile([P, N], F32, name="sg%d" % i)
+            for u in range(2):
+                nc.scalar.activation(
+                    sg_i[:, half(u)],
+                    cv_i[:].indirect(half_list(n3_t, u)),
+                    ACT.Sigmoid,
+                    bias=gate_bias[:, i : i + 1],
+                    scale=sl_t[:, i : i + 1],
+                )
+            cv.append(cv_i)
+            sg.append(sg_i)
+        for i in range(4):
+            diff = keep.tile([P, N], F32, name="diff%d" % i)
+            nc.vector.tensor_tensor(diff[:], cv[i][:], old[i][:], ALU.subtract)
+            step = keep.tile([P, N], F32, name="step%d" % i)
+            nc.vector.tensor_tensor(step[:], sg[i][:], diff[:], ALU.mult)
+            new = keep.tile([P, N], F32, name="new%d" % i)
+            nc.vector.tensor_tensor(new[:], step[:], old[i][:], ALU.add)
+            for u in range(2):
+                nc.scalar.activation(pages[i][:].indirect(half_list(n2_t, u)), new[:, half(u)], ACT.Copy)
+            nc.sync.dma_start(out[block(i), :], pages[i][:])

@@ -36,7 +36,7 @@ def tile_picked_momeshepg_none_p_kernel(
             return t
 
         def load_by_token(name, src):
-            t = keep.tile([P, PACK], F32, name=name)
+            t = keep.tile([P, PACK], F32, name=name, tag=name, align_bytes=64)
             nc.sync.dma_start(t[:], src.rearrange("(p t) o -> p (t o)", t=PACK))
             return t
 
@@ -58,19 +58,19 @@ def tile_picked_momeshepg_none_p_kernel(
 
         offs_t = load_list("offs_t", offs)
         two_t = load_list("two_t", two)
-        n2_t = load_list("n2_t", n2)
-        n1_t = load_list("n1_t", n1)
-        words = keep.tile([P, T], I32, name="words")
-        nc.sync.dma_start(words[:], x_words[0].rearrange("p c r -> p (c r)").bitcast(I32))
         sbytes = keep.tile([P, T], U8, name="sbytes")
-        nc.gpsimd.memset(sbytes[:].bitcast(I32), 0)
+        nc.vector.memset(sbytes[:].bitcast(I32), 0)
         for q in range(4):
-            nc.scalar.dma_start(
+            nc.sync.dma_start(
                 sbytes[32 * q : 32 * q + 4, :].bitcast(I32), x_scales[0, 4 * q : 4 * q + 4, :].bitcast(I32)
             )
+        words = keep.tile([P, T], I32, name="words")
+        nc.sync.dma_start(words[:], x_words[0].rearrange("p c r -> p (c r)").bitcast(I32))
         wa_raw = [load_weight("wa_raw%d" % u, wa, slice(u * HALF, (u + 1) * HALF)) for u in range(2)]
-        pages = [load_page(0)]
         tau_t = load_by_token("tau_t", tau)
+        n2_t = load_list("n2_t", n2)
+        pages = [load_page(0)]
+        n1_t = load_list("n1_t", n1)
         wb_raw = load_weight("wb_raw", wb, slice(0, N))
         gt_t = load_by_token("gt_t", gt)
         gi_t = load_by_token("gi_t", gi)
@@ -79,8 +79,8 @@ def tile_picked_momeshepg_none_p_kernel(
         sl_t = load_by_row("sl_t", sl)
         th_t = load_by_row("th_t", th)
 
-        def pick_scales(name, lst):
-            scales = keep.tile([P, S], U8, name=name, align_bytes=64)
+        def pick_scales(name, lst, tag):
+            scales = keep.tile([P, S], U8, name=name, tag=tag, align_bytes=64)
             nc.vector.tensor_copy(
                 scales[:].rearrange("p (t m) -> p m t", t=PACK), sbytes[:].indirect(lst[:])
             )
@@ -93,12 +93,10 @@ def tile_picked_momeshepg_none_p_kernel(
             )
             return codes
 
-        def round_on_gpsimd(dst, src):
-            nc.gpsimd.tensor_scalar(dst, src, 1.0, 0.0, ALU.mult, ALU.add)
 
-        def weave(name, raw, copy):
+        def weave(name, raw, copy, tag):
             width = raw.shape[2]
-            woven = keep.tile([P, width * PACK], BF16, name=name, align_bytes=64)
+            woven = keep.tile([P, width * PACK], BF16, name=name, tag=tag, align_bytes=64)
             copy(
                 woven[:].rearrange("p (c i j) -> p c j i", i=2, j=PACK),
                 raw[:].rearrange("p j (c i) -> p c j i", i=2),
@@ -132,56 +130,61 @@ def tile_picked_momeshepg_none_p_kernel(
         def half_list(lst, u):
             return lst[:, u * HALF_COLS : (u + 1) * HALF_COLS]
 
-        xa_scales = pick_scales("xa_scales", offs_t)
+        xa_scales = pick_scales("xa_scales", offs_t, "xa_scales")
         xa = (pick_codes("xa_codes", offs_t, "xa_codes"), xa_scales)
-        wa_woven = [weave("wa_woven0", wa_raw[0], nc.scalar.copy), weave("wa_woven1", wa_raw[1], nc.vector.tensor_copy)]
-        wa_q = [quantize("wa%d" % u, wa_woven[u]) for u in range(2)]
+        wa_q = [
+            quantize("wa0", weave("wa_woven0", wa_raw[0], nc.vector.tensor_copy, "wa_woven0")),
+            quantize("wa1", weave("wa_woven1", wa_raw[1], nc.vector.tensor_copy, "wa_woven1")),
+        ]
 
-        xb_scales = pick_scales("xb_scales", two_t)
-        old = [keep.tile([P, N], F32, name="old0")]
-        nc.scalar.activation(old[0][:], pages[0][:].indirect(n2_t[:]), ACT.Copy)
+        xb_scales = pick_scales("xb_scales", two_t, "xb_scales")
+        neg_tau = keep.tile([P, PACK], F32, name="neg_tau")
+        nc.scalar.activation(neg_tau[:], tau_t[:], ACT.Copy, scale=-1.0)
+        cv_window = []
 
-        top = keep.tile([P, PACK], F32, name="top", tag="top", align_bytes=64)
+        def fetch_old(i, tag):
+            window = keep.tile([P, 2 * N], F32, name="cv_window%d" % i, tag=tag, align_bytes=64)
+            nc.scalar.activation(window[:, N:], pages[i][:].indirect(n2_t[:]), ACT.Copy)
+            cv_window.append(window)
+
+        fetch_old(0, "cv_window0")
+
         shift = keep.tile([P, PACK], F32, name="shift")
         ea = keep.tile([P, PACK, H], F32, name="ea")
+        a_banks = [psum.tile([P, H], F32, name="a_bank%d" % t, tag="wide%d" % t) for t in range(PACK)]
+        for u in range(2):
+            for t in range(PACK):
+                product(a_banks[t][:, half(u)], xa, block(t), wa_q[u], slice(0, HALF))
         a = []
         for t in range(PACK):
-            bank = psum.tile([P, H], F32, name="a_bank%d" % t, tag="wide%d" % t)
-            for u in range(2):
-                product(bank[:, half(u)], xa, block(t), wa_q[u], slice(0, HALF))
-            a_t = keep.tile([P, H], F32, name="a%d" % t)
+            a_window = keep.tile([P, 2 * H], F32, name="a_window%d" % t)
+            nc.gpsimd.memset(a_window[:, H:], 0.0)
+            a_t = a_window[:, :H]
+            top = keep.tile([P, 1], F32, name="top%d" % t, tag="top%d" % t, align_bytes=64)
             nc.vector.tensor_scalar(
-                a_t[:], bank[:], 1.0, None, ALU.mult, ALU.max, accum_out=top[:, t : t + 1]
+                a_t, a_banks[t][:], 1.0, None, ALU.mult, ALU.max, accum_out=top[:]
             )
             nc.vector.tensor_scalar(
-                shift[:, t : t + 1], top[:, t : t + 1], tau_t[:, t : t + 1], -1.0, ALU.mult, ALU.mult
+                shift[:, t : t + 1], top[:], neg_tau[:, t : t + 1], None, ALU.mult
             )
-            for u in range(2):
-                nc.scalar.activation(
-                    ea[:, t, half(u)],
-                    a_t[:].indirect(half_list(n1_t, u)),
-                    ACT.Exp,
-                    bias=shift[:, t : t + 1],
-                    scale=tau_t[:, t : t + 1],
-                )
+            nc.scalar.activation(
+                ea[:, t, :],
+                a_window[:].indirect(n1_t[:]),
+                ACT.Exp,
+                bias=shift[:, t : t + 1],
+                scale=tau_t[:, t : t + 1],
+            )
             a.append(a_t)
 
-        rest = keep.tile([P, PACK, H], F32, name="rest")
-        nc.scalar.activation(rest[:], ea[:], ACT.Ln, bias=0.25)
+        rest = keep.tile([P, PACK, H], F32, name="rest", tag="rest", align_bytes=64)
+        for u in range(2):
+            nc.scalar.activation(rest[:, :, half(u)], ea[:, :, half(u)], ACT.Ln, bias=0.25)
 
-        xb = (pick_codes("xb_codes", two_t, "top"), xb_scales)
-        wb_q = quantize("wb", weave("wb_woven", wb_raw, round_on_gpsimd))
+        xb = (pick_codes("xb_codes", two_t, "top3"), xb_scales)
+        wb_q = quantize("wb", weave("wb_woven", wb_raw, nc.vector.tensor_copy, "top2"))
         ga = keep.tile([P, PACK, H], F32, name="ga")
         for t in range(PACK):
-            nc.gpsimd.tensor_scalar(ga[:, t, :], a[t][:], gt_t[:, t : t + 1], 2.0, ALU.mult, ALU.mult)
-
-        logit = keep.tile([P, PACK, H], F32, name="logit", tag="logit")
-        share = keep.tile([P, PACK, H], F32, name="share")
-        for t in range(PACK):
-            nc.vector.scalar_tensor_tensor(
-                logit[:, t, :], a[t][:], tau_t[:, t : t + 1], rest[:, t, :], ALU.mult, ALU.subtract
-            )
-            nc.scalar.activation(share[:, t, :], logit[:, t, :], ACT.Sigmoid, bias=shift[:, t : t + 1])
+            nc.vector.tensor_scalar(ga[:, t, :], a[t], gt_t[:, t : t + 1], 2.0, ALU.mult, ALU.mult)
 
         z2_woven = keep.tile([P, N * PACK], BF16, name="z2_woven", align_bytes=64)
         for i in range(4):
@@ -194,54 +197,96 @@ def tile_picked_momeshepg_none_p_kernel(
                 gi_t[:].unsqueeze(1).broadcast_to([P, P, PACK]),
                 ALU.mult,
             )
+        share = keep.tile([P, PACK, H], F32, name="share")
+        held = ("gi_t", "xb_scales")
+        for u in range(2):
+            logit = keep.tile([P, PACK, HALF], F32, name="logit%d" % u, tag=held[u], align_bytes=64)
+            for t in range(PACK):
+                nc.vector.scalar_tensor_tensor(
+                    logit[:, t, :],
+                    a[t][:, half(u)],
+                    tau_t[:, t : t + 1],
+                    rest[:, t, half(u)],
+                    ALU.mult,
+                    ALU.subtract,
+                )
+                nc.scalar.activation(
+                    share[:, t, half(u)], logit[:, t, :], ACT.Sigmoid, bias=shift[:, t : t + 1]
+                )
         z2_q = quantize("z2", z2_woven)
 
-        old_rest = keep.tile([P, 3, N], F32, name="old_rest", tag="logit")
-        for i in range(1, 4):
-            nc.scalar.activation(old_rest[:, i - 1, :], pages[i][:].indirect(n2_t[:]), ACT.Copy)
-            old.append(old_rest[:, i - 1, :])
+        fetch_old(1, "rest")
+        fetch_old(2, held[0])
+        fetch_old(3, held[1])
 
         gate_bias = keep.tile([P, PACK], F32, name="gate_bias")
         slope_th = keep.tile([P, PACK], F32, name="slope_th")
         nc.gpsimd.tensor_tensor(slope_th[:], sl_t[:], th_t[:], ALU.mult)
         nc.gpsimd.tensor_scalar(gate_bias[:], slope_th[:], -1.0, 0.0, ALU.mult, ALU.add)
 
-        cv_banks = []
-        cv = []
-        sg = []
-        for i in range(4):
-            z_woven = keep.tile([P, P * PACK], BF16, name="z_woven%d" % i, align_bytes=64)
+        z_woven, cv_banks, sg, diff, step, new = {}, {}, {}, {}, {}, {}
+
+        def weigh(i):
+            z_woven[i] = keep.tile([P, P * PACK], BF16, name="z_woven%d" % i, align_bytes=64)
             nc.vector.tensor_tensor(
-                z_woven[:].rearrange("p (c e t) -> p c t e", e=2, t=PACK),
+                z_woven[i][:].rearrange("p (c e t) -> p c t e", e=2, t=PACK),
                 ga[:, :, block(i)].rearrange("p t (c e) -> p c t e", e=2),
                 share[:, :, block(i)].rearrange("p t (c e) -> p c t e", e=2),
                 ALU.mult,
             )
-            z_q = quantize("z_block%d" % i, z_woven)
-            bank = psum.tile([P, N], F32, name="cv_bank%d" % i, tag="wide%d" % i)
-            product(bank[:], z_q, slice(0, P), z2_q, slice(0, N))
-            cv_banks.append(bank)
-        for i in range(4):
-            cv_i = keep.tile([P, N], F32, name="cv%d" % i)
-            nc.vector.tensor_scalar(cv_i[:], cv_banks[i][:], 0.0625, None, ALU.mult)
-            sg_i = keep.tile([P, N], F32, name="sg%d" % i)
+
+        def moments(i):
+            z_q = quantize("z_block%d" % i, z_woven[i])
+            cv_banks[i] = psum.tile([P, N], F32, name="cv_bank%d" % i, tag="wide%d" % i)
+            product(cv_banks[i][:], z_q, slice(0, P), z2_q, slice(0, N))
+
+        def gate(i):
+            nc.vector.tensor_scalar(cv_window[i][:, :N], cv_banks[i][:], 0.0625, None, ALU.mult)
+            sg[i] = keep.tile([P, N], F32, name="sg%d" % i)
+            nc.scalar.activation(
+                sg[i][:],
+                cv_window[i][:].indirect(n3_t[:]),
+                ACT.Sigmoid,
+                bias=gate_bias[:, i : i + 1],
+                scale=sl_t[:, i : i + 1],
+            )
+
+        def take_diff(i):
+            diff[i] = keep.tile([P, N], F32, name="diff%d" % i)
+            nc.vector.tensor_tensor(diff[i][:], cv_window[i][:, :N], cv_window[i][:, N:], ALU.subtract)
+
+        def take_step(i):
+            step[i] = keep.tile([P, N], F32, name="step%d" % i)
+            nc.vector.tensor_tensor(step[i][:], sg[i][:], diff[i][:], ALU.mult)
+
+        def take_new(i):
+            new[i] = keep.tile([P, N], F32, name="new%d" % i)
+            nc.vector.tensor_tensor(new[i][:], step[i][:], cv_window[i][:, N:], ALU.add)
+
+        weigh(0)
+        weigh(1)
+        moments(0)
+        moments(1)
+        weigh(2)
+        gate(0)
+        weigh(3)
+        gate(1)
+        moments(2)
+        moments(3)
+        take_diff(0)
+        gate(2)
+        take_step(0)
+        gate(3)
+        take_new(0)
+        for i in range(1, 4):
+            take_diff(i)
+            take_step(i)
+            take_new(i)
+        for pair in ((0, 1), (2, 3)):
             for u in range(2):
-                nc.scalar.activation(
-                    sg_i[:, half(u)],
-                    cv_i[:].indirect(half_list(n3_t, u)),
-                    ACT.Sigmoid,
-                    bias=gate_bias[:, i : i + 1],
-                    scale=sl_t[:, i : i + 1],
-                )
-            cv.append(cv_i)
-            sg.append(sg_i)
-        for i in range(4):
-            diff = keep.tile([P, N], F32, name="diff%d" % i)
-            nc.vector.tensor_tensor(diff[:], cv[i][:], old[i][:], ALU.subtract)
-            step = keep.tile([P, N], F32, name="step%d" % i)
-            nc.vector.tensor_tensor(step[:], sg[i][:], diff[:], ALU.mult)
-            new = keep.tile([P, N], F32, name="new%d" % i)
-            nc.vector.tensor_tensor(new[:], step[:], old[i][:], ALU.add)
-            for u in range(2):
-                nc.scalar.activation(pages[i][:].indirect(half_list(n2_t, u)), new[:, half(u)], ACT.Copy)
-            nc.sync.dma_start(out[block(i), :], pages[i][:])
+                for i in pair:
+                    nc.scalar.activation(
+                        pages[i][:].indirect(half_list(n2_t, u)), new[i][:, half(u)], ACT.Copy
+                    )
+            for i in pair:
+                nc.sync.dma_start(out[block(i), :], pages[i][:])

@@ -46,9 +46,9 @@ def tile_picked_momeshepg_none_p_kernel(
                 nc.sync.dma_start(t[:], src.rearrange("(i p) o -> p (i o)", p=P))
             return t
 
-        def load_weight(name, src, cols):
-            t = keep.tile([P, PACK, cols.stop - cols.start], F32, name=name)
-            nc.sync.dma_start(t[:], src.rearrange("(p j) c -> p j c", j=PACK)[:, :, cols])
+        def load_weight(name, src):
+            t = keep.tile([P, PACK, H], F32, name=name)
+            nc.sync.dma_start(t[:], src.rearrange("(p j) c -> p j c", j=PACK))
             return t
 
         def load_page(i):
@@ -64,14 +64,14 @@ def tile_picked_momeshepg_none_p_kernel(
             nc.sync.dma_start(
                 sbytes[32 * q : 32 * q + 4, :].bitcast(I32), x_scales[0, 4 * q : 4 * q + 4, :].bitcast(I32)
             )
+        wa_raw = load_weight("wa_raw", wa)
         words = keep.tile([P, T], I32, name="words")
         nc.sync.dma_start(words[:], x_words[0].rearrange("p c r -> p (c r)").bitcast(I32))
-        wa_raw = [load_weight("wa_raw%d" % u, wa, slice(u * HALF, (u + 1) * HALF)) for u in range(2)]
         tau_t = load_by_token("tau_t", tau)
         n2_t = load_list("n2_t", n2)
         pages = [load_page(0)]
         n1_t = load_list("n1_t", n1)
-        wb_raw = load_weight("wb_raw", wb, slice(0, N))
+        wb_raw = load_weight("wb_raw", wb)
         gt_t = load_by_token("gt_t", gt)
         gi_t = load_by_token("gi_t", gi)
         pages.extend(load_page(i) for i in range(1, 4))
@@ -94,21 +94,22 @@ def tile_picked_momeshepg_none_p_kernel(
             return codes
 
 
-        def weave(name, raw, copy, tag):
-            width = raw.shape[2]
-            woven = keep.tile([P, width * PACK], BF16, name=name, tag=tag, align_bytes=64)
-            copy(
-                woven[:].rearrange("p (c i j) -> p c j i", i=2, j=PACK),
-                raw[:].rearrange("p j (c i) -> p c j i", i=2),
+        def weave(woven, raw):
+            nc.vector.tensor_copy(
+                woven.rearrange("p (c i j) -> p c j i", i=2, j=PACK),
+                raw.rearrange("p j (c i) -> p c j i", i=2),
             )
-            return woven
 
-        def quantize(name, woven):
-            width = woven.shape[1] // PACK
+        def mx_tiles(name, width):
             codes = keep.tile([P, width], U32, name=name + "_codes", align_bytes=64)
             scales = keep.tile([P, width], U8, name=name + "_scales", align_bytes=64)
-            nc.vector.quantize_mx(out=codes[:].bitcast(FP8X4), scales=scales[:], in_=woven[:])
             return codes, scales
+
+        def quantize(dst, cols, woven):
+            nc.vector.quantize_mx(out=dst[0][:, cols].bitcast(FP8X4), scales=dst[1][:, cols], in_=woven)
+
+        def woven_half(u):
+            return slice(u * HALF * PACK, (u + 1) * HALF * PACK)
 
         def product(dst, lhs, lcols, rhs, rcols):
             nc.tensor.matmul_mx(
@@ -131,14 +132,15 @@ def tile_picked_momeshepg_none_p_kernel(
             return lst[:, u * HALF_COLS : (u + 1) * HALF_COLS]
 
         xa_scales = pick_scales("xa_scales", offs_t, "xa_scales")
-        xa = (pick_codes("xa_codes", offs_t, "xa_codes"), xa_scales)
-        wa_q = [
-            quantize("wa0", weave("wa_woven0", wa_raw[0], nc.vector.tensor_copy, "wa_woven0")),
-            quantize("wa1", weave("wa_woven1", wa_raw[1], nc.vector.tensor_copy, "wa_woven1")),
-        ]
-
         xb_scales = pick_scales("xb_scales", two_t, "xb_scales")
-        neg_tau = keep.tile([P, PACK], F32, name="neg_tau")
+        wa_woven = keep.tile([P, H * PACK], BF16, name="wa_woven", align_bytes=64)
+        weave(wa_woven[:], wa_raw[:])
+        wa_q = mx_tiles("wa", H)
+        quantize(wa_q, slice(0, H), wa_woven[:])
+        xa = (pick_codes("xa_codes", offs_t, "xa_codes"), xa_scales)
+        xb = (pick_codes("xb_codes", two_t, "xb_codes"), xb_scales)
+
+        neg_tau = keep.tile([P, PACK], F32, name="neg_tau", tag="neg_tau", align_bytes=64)
         nc.scalar.activation(neg_tau[:], tau_t[:], ACT.Copy, scale=-1.0)
         cv_window = []
 
@@ -149,23 +151,22 @@ def tile_picked_momeshepg_none_p_kernel(
 
         fetch_old(0, "cv_window0")
 
-        shift = keep.tile([P, PACK], F32, name="shift")
+        top = keep.tile([P, PACK], F32, name="top")
+        shift = keep.tile([P, PACK], F32, name="shift", tag="shift", align_bytes=64)
         ea = keep.tile([P, PACK, H], F32, name="ea")
         a_banks = [psum.tile([P, H], F32, name="a_bank%d" % t, tag="wide%d" % t) for t in range(PACK)]
-        for u in range(2):
-            for t in range(PACK):
-                product(a_banks[t][:, half(u)], xa, block(t), wa_q[u], slice(0, HALF))
+        for t in range(PACK):
+            product(a_banks[t][:], xa, block(t), wa_q, slice(0, H))
         a = []
         for t in range(PACK):
             a_window = keep.tile([P, 2 * H], F32, name="a_window%d" % t)
             nc.gpsimd.memset(a_window[:, H:], 0.0)
             a_t = a_window[:, :H]
-            top = keep.tile([P, 1], F32, name="top%d" % t, tag="top%d" % t, align_bytes=64)
             nc.vector.tensor_scalar(
-                a_t, a_banks[t][:], 1.0, None, ALU.mult, ALU.max, accum_out=top[:]
+                a_t, a_banks[t][:], 1.0, None, ALU.mult, ALU.max, accum_out=top[:, t : t + 1]
             )
-            nc.vector.tensor_scalar(
-                shift[:, t : t + 1], top[:], neg_tau[:, t : t + 1], None, ALU.mult
+            nc.scalar.activation(
+                shift[:, t : t + 1], top[:, t : t + 1], ACT.Copy, scale=neg_tau[:, t : t + 1]
             )
             nc.scalar.activation(
                 ea[:, t, :],
@@ -180,11 +181,14 @@ def tile_picked_momeshepg_none_p_kernel(
         for u in range(2):
             nc.scalar.activation(rest[:, :, half(u)], ea[:, :, half(u)], ACT.Ln, bias=0.25)
 
-        xb = (pick_codes("xb_codes", two_t, "top3"), xb_scales)
-        wb_q = quantize("wb", weave("wb_woven", wb_raw, nc.vector.tensor_copy, "top2"))
+        wb_woven = keep.tile([P, N * PACK], BF16, name="wb_woven", tag="neg_tau", align_bytes=64)
+        wb_q = mx_tiles("wb", N)
+        for u in range(2):
+            weave(wb_woven[:, woven_half(u)], wb_raw[:, :, half(u)])
+            quantize(wb_q, half(u), wb_woven[:, woven_half(u)])
         ga = keep.tile([P, PACK, H], F32, name="ga")
         for t in range(PACK):
-            nc.vector.tensor_scalar(ga[:, t, :], a[t], gt_t[:, t : t + 1], 2.0, ALU.mult, ALU.mult)
+            nc.gpsimd.tensor_scalar(ga[:, t, :], a[t], gt_t[:, t : t + 1], 2.0, ALU.mult, ALU.mult)
 
         z2_woven = keep.tile([P, N * PACK], BF16, name="z2_woven", align_bytes=64)
         for i in range(4):
@@ -213,11 +217,12 @@ def tile_picked_momeshepg_none_p_kernel(
                 nc.scalar.activation(
                     share[:, t, half(u)], logit[:, t, :], ACT.Sigmoid, bias=shift[:, t : t + 1]
                 )
-        z2_q = quantize("z2", z2_woven)
+        z2_q = mx_tiles("z2", N)
+        quantize(z2_q, slice(0, N), z2_woven[:])
 
         fetch_old(1, "rest")
-        fetch_old(2, held[0])
-        fetch_old(3, held[1])
+        fetch_old(2, held[1])
+        fetch_old(3, "shift")
 
         gate_bias = keep.tile([P, PACK], F32, name="gate_bias")
         slope_th = keep.tile([P, PACK], F32, name="slope_th")
@@ -236,7 +241,8 @@ def tile_picked_momeshepg_none_p_kernel(
             )
 
         def moments(i):
-            z_q = quantize("z_block%d" % i, z_woven[i])
+            z_q = mx_tiles("z_block%d" % i, P)
+            quantize(z_q, slice(0, P), z_woven[i][:])
             cv_banks[i] = psum.tile([P, N], F32, name="cv_bank%d" % i, tag="wide%d" % i)
             product(cv_banks[i][:], z_q, slice(0, P), z2_q, slice(0, N))
 

@@ -160,7 +160,7 @@ def tile_picked_momeshepg_none_p_kernel(
         a = []
         for t in range(PACK):
             a_window = keep.tile([P, 2 * H], F32, name="a_window%d" % t)
-            nc.gpsimd.memset(a_window[:, H:], 0.0)
+            nc.vector.memset(a_window[:, H:], 0.0)
             a_t = a_window[:, :H]
             nc.vector.tensor_scalar(
                 a_t, a_banks[t][:], 1.0, None, ALU.mult, ALU.max, accum_out=top[:, t : t + 1]
@@ -177,7 +177,7 @@ def tile_picked_momeshepg_none_p_kernel(
             )
             a.append(a_t)
 
-        rest = keep.tile([P, PACK, H], F32, name="rest", tag="rest", align_bytes=64)
+        rest = keep.tile([P, PACK, H], F32, name="rest")
         for u in range(2):
             nc.scalar.activation(rest[:, :, half(u)], ea[:, :, half(u)], ACT.Ln, bias=0.25)
 
@@ -188,7 +188,7 @@ def tile_picked_momeshepg_none_p_kernel(
             quantize(wb_q, half(u), wb_woven[:, woven_half(u)])
         ga = keep.tile([P, PACK, H], F32, name="ga")
         for t in range(PACK):
-            nc.gpsimd.tensor_scalar(ga[:, t, :], a[t], gt_t[:, t : t + 1], 2.0, ALU.mult, ALU.mult)
+            nc.vector.tensor_scalar(ga[:, t, :], a[t], gt_t[:, t : t + 1], 2.0, ALU.mult, ALU.mult)
 
         z2_woven = keep.tile([P, N * PACK], BF16, name="z2_woven", align_bytes=64)
         for i in range(4):
@@ -220,9 +220,8 @@ def tile_picked_momeshepg_none_p_kernel(
         z2_q = mx_tiles("z2", N)
         quantize(z2_q, slice(0, N), z2_woven[:])
 
-        fetch_old(1, "rest")
-        fetch_old(2, held[1])
-        fetch_old(3, "shift")
+        fetch_old(1, held[1])
+        fetch_old(2, "shift")
 
         gate_bias = keep.tile([P, PACK], F32, name="gate_bias")
         slope_th = keep.tile([P, PACK], F32, name="slope_th")
@@ -232,7 +231,7 @@ def tile_picked_momeshepg_none_p_kernel(
         z_woven, cv_banks, sg, diff, step, new = {}, {}, {}, {}, {}, {}
 
         def weigh(i):
-            z_woven[i] = keep.tile([P, P * PACK], BF16, name="z_woven%d" % i, align_bytes=64)
+            z_woven[i] = keep.tile([P, P * PACK], BF16, name="z_woven%d" % i, tag="z_woven%d" % i, align_bytes=64)
             nc.vector.tensor_tensor(
                 z_woven[i][:].rearrange("p (c e t) -> p c t e", e=2, t=PACK),
                 ga[:, :, block(i)].rearrange("p t (c e) -> p c t e", e=2),
@@ -272,6 +271,7 @@ def tile_picked_momeshepg_none_p_kernel(
         weigh(0)
         weigh(1)
         moments(0)
+        fetch_old(3, "z_woven0")
         moments(1)
         weigh(2)
         gate(0)

from contextlib import ExitStack

import concourse.mybir as mybir

K, T, S, N, H, U = 512, 2048, 512, 512, 512, 1024
FLOPS = 2 * K * S * H + 2 * K * S * N + 2 * S * H * N

F32 = mybir.dt.float32
BF16 = mybir.dt.bfloat16
I32 = mybir.dt.int32
U32 = mybir.dt.uint32
U16 = mybir.dt.uint16
U8 = mybir.dt.uint8
FP8X4 = mybir.dt.float8_e4m3fn_x4
ALU = mybir.AluOpType
ACT = mybir.ActivationFunctionType

P = 128
PACK = 4
HALF = 256
LIST_COLS = 32
HALF_COLS = 16


def tile_picked_momeshepg_none_p_kernel(
    tc, x_words, x_scales, wa, wb, tau, gt, gi, mem, sl, th, offs, two, n1, n2, n3, out
):
    nc = tc.nc
    with ExitStack() as ctx:
        keep = ctx.enter_context(tc.tile_pool(name="keep", bufs=1))
        psum = ctx.enter_context(tc.psum_pool(name="psum", bufs=1))

        def load_list(name, src):
            t = keep.tile([P, LIST_COLS], U16, name=name)
            nc.sync.dma_start(t[:], src)
            return t

        def load_by_token(name, src):
            t = keep.tile([P, PACK], F32, name=name, tag=name, align_bytes=64)
            nc.sync.dma_start(t[:], src.rearrange("(p t) o -> p (t o)", t=PACK))
            return t

        def load_by_row(name, src):
            t = keep.tile([P, PACK], F32, name=name)
            with nc.allow_non_contiguous_dma(reason="one value a partition and row block"):
                nc.sync.dma_start(t[:], src.rearrange("(i p) o -> p (i o)", p=P))
            return t

        def load_weight(name, src):
            t = keep.tile([P, PACK, H], F32, name=name)
            nc.sync.dma_start(t[:], src.rearrange("(p j) c -> p j c", j=PACK))
            return t

        def load_page(i):
            t = keep.tile([P, U], F32, name="page%d" % i)
            nc.sync.dma_start(t[:], mem[i * P : (i + 1) * P, :])
            return t

        offs_t = load_list("offs_t", offs)
        two_t = load_list("two_t", two)
        sbytes = keep.tile([P, T], U8, name="sbytes")
        nc.vector.memset(sbytes[:].bitcast(I32), 0)
        for q in range(4):
            nc.sync.dma_start(
                sbytes[32 * q : 32 * q + 4, :].bitcast(I32), x_scales[0, 4 * q : 4 * q + 4, :].bitcast(I32)
            )
        wa_raw = load_weight("wa_raw", wa)
        words = keep.tile([P, T], I32, name="words")
        nc.sync.dma_start(words[:], x_words[0].rearrange("p c r -> p (c r)").bitcast(I32))
        tau_t = load_by_token("tau_t", tau)
        n2_t = load_list("n2_t", n2)
        pages = [load_page(0)]
        n1_t = load_list("n1_t", n1)
        wb_raw = load_weight("wb_raw", wb)
        gt_t = load_by_token("gt_t", gt)
        gi_t = load_by_token("gi_t", gi)
        pages.extend(load_page(i) for i in range(1, 4))
        n3_t = load_list("n3_t", n3)
        sl_t = load_by_row("sl_t", sl)
        th_t = load_by_row("th_t", th)

        def pick_scales(name, lst, tag):
            scales = keep.tile([P, S], U8, name=name, tag=tag, align_bytes=64)
            nc.vector.tensor_copy(
                scales[:].rearrange("p (t m) -> p m t", t=PACK), sbytes[:].indirect(lst[:])
            )
            return scales

        def pick_codes(name, lst, tag):
            codes = keep.tile([P, S], U32, name=name, tag=tag, align_bytes=64)
            nc.vector.tensor_copy(
                codes[:].rearrange("p (t m) -> p m t", t=PACK), words[:].bitcast(U32).indirect(lst[:])
            )
            return codes


        def weave(woven, raw):
            nc.vector.tensor_copy(
                woven.rearrange("p (c i j) -> p c j i", i=2, j=PACK),
                raw.rearrange("p j (c i) -> p c j i", i=2),
            )

        def mx_tiles(name, width):
            codes = keep.tile([P, width], U32, name=name + "_codes", align_bytes=64)
            scales = keep.tile([P, width], U8, name=name + "_scales", align_bytes=64)
            return codes, scales

        def quantize(dst, cols, woven):
            nc.vector.quantize_mx(out=dst[0][:, cols].bitcast(FP8X4), scales=dst[1][:, cols], in_=woven)

        def woven_half(u):
            return slice(u * HALF * PACK, (u + 1) * HALF * PACK)

        def product(dst, lhs, lcols, rhs, rcols):
            nc.tensor.matmul_mx(
                out=dst,
                lhsT=lhs[0][:, lcols].bitcast(FP8X4),
                lhsT_scale=lhs[1][:, lcols],
                rhs=rhs[0][:, rcols].bitcast(FP8X4),
                rhs_scale=rhs[1][:, rcols],
                start=True,
                stop=True,
            )

        def block(i):
            return slice(i * P, (i + 1) * P)

        def half(u):
            return slice(u * HALF, (u + 1) * HALF)

        def half_list(lst, u):
            return lst[:, u * HALF_COLS : (u + 1) * HALF_COLS]

        xa_scales = pick_scales("xa_scales", offs_t, "xa_scales")
        xb_scales = pick_scales("xb_scales", two_t, "xb_scales")
        wa_woven = keep.tile([P, H * PACK], BF16, name="wa_woven", align_bytes=64)
        weave(wa_woven[:], wa_raw[:])
        wa_q = mx_tiles("wa", H)
        quantize(wa_q, slice(0, H), wa_woven[:])
        xa = (pick_codes("xa_codes", offs_t, "xa_codes"), xa_scales)
        xb = (pick_codes("xb_codes", two_t, "xb_codes"), xb_scales)

        neg_tau = keep.tile([P, PACK], F32, name="neg_tau", tag="neg_tau", align_bytes=64)
        nc.scalar.activation(neg_tau[:], tau_t[:], ACT.Copy, scale=-1.0)
        cv_window = []

        def fetch_old(i, tag):
            window = keep.tile([P, 2 * N], F32, name="cv_window%d" % i, tag=tag, align_bytes=64)
            nc.scalar.activation(window[:, N:], pages[i][:].indirect(n2_t[:]), ACT.Copy)
            cv_window.append(window)

        fetch_old(0, "cv_window0")

        top = keep.tile([P, PACK], F32, name="top")
        shift = keep.tile([P, PACK], F32, name="shift", tag="shift", align_bytes=64)
        ea = keep.tile([P, PACK, H], F32, name="ea")
        a_banks = [psum.tile([P, H], F32, name="a_bank%d" % t, tag="wide%d" % t) for t in range(PACK)]
        for t in range(PACK):
            product(a_banks[t][:], xa, block(t), wa_q, slice(0, H))
        a = []
        for t in range(PACK):
            a_window = keep.tile([P, 2 * H], F32, name="a_window%d" % t)
            nc.vector.memset(a_window[:, H:], 0.0)
            a_t = a_window[:, :H]
            nc.vector.tensor_scalar(
                a_t, a_banks[t][:], 1.0, None, ALU.mult, ALU.max, accum_out=top[:, t : t + 1]
            )
            nc.scalar.activation(
                shift[:, t : t + 1], top[:, t : t + 1], ACT.Copy, scale=neg_tau[:, t : t + 1]
            )
            nc.scalar.activation(
                ea[:, t, :],
                a_window[:].indirect(n1_t[:]),
                ACT.Exp,
                bias=shift[:, t : t + 1],
                scale=tau_t[:, t : t + 1],
            )
            a.append(a_t)

        rest = keep.tile([P, PACK, H], F32, name="rest")
        for u in range(2):
            nc.scalar.activation(rest[:, :, half(u)], ea[:, :, half(u)], ACT.Ln, bias=0.25)

        wb_woven = keep.tile([P, N * PACK], BF16, name="wb_woven", tag="neg_tau", align_bytes=64)
        wb_q = mx_tiles("wb", N)
        for u in range(2):
            weave(wb_woven[:, woven_half(u)], wb_raw[:, :, half(u)])
            quantize(wb_q, half(u), wb_woven[:, woven_half(u)])
        ga = keep.tile([P, PACK, H], F32, name="ga")
        for t in range(PACK):
            nc.vector.tensor_scalar(ga[:, t, :], a[t], gt_t[:, t : t + 1], 2.0, ALU.mult, ALU.mult)

        z2_woven = keep.tile([P, N * PACK], BF16, name="z2_woven", align_bytes=64)
        for i in range(4):
            bank = psum.tile([P, PACK, P], F32, name="b_bank%d" % i)
            for t in range(PACK):
                product(bank[:, t, :], xb, block(t), wb_q, block(i))
            nc.vector.tensor_tensor(
                z2_woven[:, i * P * PACK : (i + 1) * P * PACK].rearrange("p (n t) -> p n t", t=PACK),
                bank[:].rearrange("p t n -> p n t"),
                gi_t[:].unsqueeze(1).broadcast_to([P, P, PACK]),
                ALU.mult,
            )
        share = keep.tile([P, PACK, H], F32, name="share")
        held = ("gi_t", "xb_scales")
        for u in range(2):
            logit = keep.tile([P, PACK, HALF], F32, name="logit%d" % u, tag=held[u], align_bytes=64)
            for t in range(PACK):
                nc.vector.scalar_tensor_tensor(
                    logit[:, t, :],
                    a[t][:, half(u)],
                    tau_t[:, t : t + 1],
                    rest[:, t, half(u)],
                    ALU.mult,
                    ALU.subtract,
                )
                nc.scalar.activation(
                    share[:, t, half(u)], logit[:, t, :], ACT.Sigmoid, bias=shift[:, t : t + 1]
                )
        z2_q = mx_tiles("z2", N)
        quantize(z2_q, slice(0, N), z2_woven[:])

        fetch_old(1, held[1])
        fetch_old(2, "shift")

        gate_bias = keep.tile([P, PACK], F32, name="gate_bias")
        slope_th = keep.tile([P, PACK], F32, name="slope_th")
        nc.gpsimd.tensor_tensor(slope_th[:], sl_t[:], th_t[:], ALU.mult)
        nc.gpsimd.tensor_scalar(gate_bias[:], slope_th[:], -1.0, 0.0, ALU.mult, ALU.add)

        z_woven, cv_banks, sg, diff, step, new = {}, {}, {}, {}, {}, {}

        def weigh(i):
            z_woven[i] = keep.tile([P, P * PACK], BF16, name="z_woven%d" % i, tag="z_woven%d" % i, align_bytes=64)
            nc.vector.tensor_tensor(
                z_woven[i][:].rearrange("p (c e t) -> p c t e", e=2, t=PACK),
                ga[:, :, block(i)].rearrange("p t (c e) -> p c t e", e=2),
                share[:, :, block(i)].rearrange("p t (c e) -> p c t e", e=2),
                ALU.mult,
            )

        def moments(i):
            z_q = mx_tiles("z_block%d" % i, P)
            quantize(z_q, slice(0, P), z_woven[i][:])
            cv_banks[i] = psum.tile([P, N], F32, name="cv_bank%d" % i, tag="wide%d" % i)
            product(cv_banks[i][:], z_q, slice(0, P), z2_q, slice(0, N))

        def gate(i):
            nc.vector.tensor_scalar(cv_window[i][:, :N], cv_banks[i][:], 0.0625, None, ALU.mult)
            sg[i] = keep.tile([P, N], F32, name="sg%d" % i)
            nc.scalar.activation(
                sg[i][:],
                cv_window[i][:].indirect(n3_t[:]),
                ACT.Sigmoid,
                bias=gate_bias[:, i : i + 1],
                scale=sl_t[:, i : i + 1],
            )

        def take_diff(i):
            diff[i] = keep.tile([P, N], F32, name="diff%d" % i)
            nc.vector.tensor_tensor(diff[i][:], cv_window[i][:, :N], cv_window[i][:, N:], ALU.subtract)

        def take_step(i):
            step[i] = keep.tile([P, N], F32, name="step%d" % i)
            nc.vector.tensor_tensor(step[i][:], sg[i][:], diff[i][:], ALU.mult)

        def take_new(i):
            new[i] = keep.tile([P, N], F32, name="new%d" % i)
            nc.vector.tensor_tensor(new[i][:], step[i][:], cv_window[i][:, N:], ALU.add)

        weigh(0)
        weigh(1)
        moments(0)
        fetch_old(3, "z_woven0")
        moments(1)
        weigh(2)
        gate(0)
        weigh(3)
        gate(1)
        moments(2)
        moments(3)
        take_diff(0)
        gate(2)
        take_step(0)
        gate(3)
        take_new(0)
        for i in range(1, 4):
            take_diff(i)
            take_step(i)
            take_new(i)
        for pair in ((0, 1), (2, 3)):
            for u in range(2):
                for i in pair:
                    nc.scalar.activation(
                        pages[i][:].indirect(half_list(n2_t, u)), new[i][:, half(u)], ACT.Copy
                    )
            for i in pair:
                nc.sync.dma_start(out[block(i), :], pages[i][:])
